import numpy as np
import ml_dtypes


def mxq(x, axis, fmt="e4m3"):
    dtype, down = {"e4m3": (ml_dtypes.float8_e4m3fn, 7), "e5m2": (ml_dtypes.float8_e5m2, 14)}[fmt]
    v = np.moveaxis(np.asarray(x, np.float32).astype(ml_dtypes.bfloat16).astype(np.float64), axis, -1)
    blocks = v.reshape(v.shape[:-1] + (-1, 32))
    amax = np.abs(blocks).max(-1, keepdims=True)
    byte = np.maximum(np.where(amax > 0, np.frexp(amax)[1] - 1 + 127, 0) - down, 1)
    scale = np.exp2(byte - 127.0)
    codes = (blocks / scale).astype(np.float32).astype(dtype).astype(np.float64)
    return np.moveaxis((codes * scale).reshape(v.shape), -1, axis)


WIDE = False


def mx_kscale(k):
    if not WIDE:
        return np.ones(k)
    levels = np.array([10, -10, 5, -5, 0])
    if k % 512:
        return np.exp2(np.random.permutation(np.resize(levels, k // 32))).repeat(32)
    a = np.empty((k // 512, 16))
    for p in range(k // 512):
        a[p, :8] = np.random.permutation(np.resize(levels, 8))
        for g in range(8):
            far = levels[np.abs(levels - a[p, g]) >= 10]
            a[p, g + 8] = far[np.random.randint(len(far))]
    return np.exp2(a.ravel()).repeat(32)


def f64(x):
    return np.asarray(x).astype(np.float64)


def striped(idx):
    return np.tile(np.asarray(idx).reshape(-1, 16).T, (8, 1)).astype(np.uint16)


def unstriped(offs):
    return offs[:16].T.reshape(-1).astype(np.int64)


B, N, T, D, DV, NQ = 1, 512, 1024, 512, 256, 128
NEW = 128


def setup_inputs():
    n = np.random.standard_normal
    idx = np.random.permutation(T)[:B * N]
    s = mx_kscale(D)[:, None]
    u = np.ones(T)
    u[idx] = mx_kscale(B * N)
    r = np.random.uniform(0.5, 2.0, T)
    rk = np.random.uniform(0.5, 2.0, T)
    k = n((D, T)) / s / rk
    v = n((DV, T)) / (u * r)
    new = np.random.permutation(idx.reshape(B, N)[:, -NEW // B:].reshape(-1))
    return {
        "qT": (n((B, D, NQ)) * s * (0.60 / np.sqrt(D))).astype(np.float32),
        "kT": np.where(np.isin(np.arange(T), new)[None, :], n((D, T)), k).astype(np.float32),
        "vT": np.where(np.isin(np.arange(T), new)[None, :], n((DV, T)), v).astype(np.float32),
        "new_kT": k[:, new].astype(np.float32),
        "new_vT": v[:, new].astype(np.float32),
        "ks": np.tile(rk, (128, 1)).astype(np.float32),
        "vs": np.tile(u * r, (128, 1)).astype(np.float32),
        "offs": striped(idx),
        "slots": striped(new),
    }


def reference(qT, kT, vT, new_kT, new_vT, ks, vs, offs, slots):
    idx = unstriped(offs)
    k = f64(kT)
    k[:, unstriped(slots)] = f64(new_kT)
    v = f64(vT)
    v[:, unstriped(slots)] = f64(new_vT)
    pick = lambda x: x[:, idx].reshape(x.shape[0], B, N).transpose(1, 0, 2)
    q = f64(qT)
    score = mxq(q, 1, "e4m3").transpose(0, 2, 1) @ mxq(pick(k), 1, "e4m3")
    score = score * pick(f64(ks))[:, :1, :]
    m = score.max(-1, keepdims=True)
    p = np.exp(score - m)
    total = p.sum(-1, keepdims=True)
    w = p * pick(f64(vs))[:, :1, :]
    y = mxq(w, 2, "e4m3") @ mxq(pick(v).transpose(0, 2, 1), 1, "e4m3")
    y = y / total
    return y

@@ -1,0 +1,184 @@
+from contextlib import ExitStack
+
+import concourse.mybir as mybir
+from concourse.masks import make_identity
+
+F32 = mybir.dt.float32
+BF16 = mybir.dt.bfloat16
+U32 = mybir.dt.uint32
+U16 = mybir.dt.uint16
+U8 = mybir.dt.uint8
+FP8X4 = mybir.dt.float8_e4m3fn_x4
+ACT = mybir.ActivationFunctionType
+ALU = mybir.AluOpType
+AX = mybir.AxisListType
+
+P = 128
+PACK = 4
+T = 1024
+N = 512
+NQ = 128
+DV = 256
+NEW = 128
+HALF = N // 2
+FLOPS = 2 * NQ * N * 512 + 2 * NQ * N * DV
+
+
+def tile_attend_x_ks_append128_topk_kernel(tc, qT, kT, vT, new_kT, new_vT, ks, vs, offs, slots, out):
+    nc = tc.nc
+    with ExitStack() as ctx:
+        keep = ctx.enter_context(tc.tile_pool(name="keep", bufs=1))
+        psum = ctx.enter_context(tc.psum_pool(name="psum", bufs=1))
+
+        kview = kT.rearrange("(p t) n -> p t n", t=PACK)
+        newk = keep.tile([P, PACK, NEW], F32, name="newk")
+        newv = keep.tile([P, 2, NEW], F32, name="newv")
+        place = keep.tile([P, NEW // 16], U16, name="place")
+        idx = keep.tile([P, N // 16], U16, name="idx")
+        kp = []
+        vp = []
+        for t in range(PACK):
+            kp.append(keep.tile([P, T], F32, name="kpool%d" % t))
+        for b in range(2):
+            vp.append(keep.tile([P, T], F32, name="vpool%d" % b))
+        q_sb = keep.tile([P, PACK, NQ], F32, name="q_sb")
+        ks_sb = keep.tile([P, T], F32, name="ks_sb")
+        vs_sb = keep.tile([P, T], F32, name="vs_sb")
+        nc.sync.dma_start(newk[:], new_kT.rearrange("(p t) n -> p t n", t=PACK))
+        nc.sync.dma_start(kp[2][:], kview[:, 2, :])
+        nc.sync.dma_start(place[:], slots)
+        nc.sync.dma_start(idx[:], offs)
+        nc.sync.dma_start(ks_sb[:], ks)
+        nc.sync.dma_start(kp[3][:], kview[:, 3, :])
+        nc.sync.dma_start(q_sb[:], qT[0].rearrange("(p t) q -> p t q", t=PACK))
+        nc.sync.dma_start(newv[:], new_vT.rearrange("(b p) n -> p b n", b=2))
+        nc.sync.dma_start(vp[0][:], vT[0:P, :])
+        nc.sync.dma_start(vs_sb[:], vs)
+        nc.sync.dma_start(vp[1][:], vT[P : 2 * P, :])
+        nc.sync.dma_start(kp[0][:], kview[:, 0, :])
+        nc.sync.dma_start(kp[1][:], kview[:, 1, :])
+
+        ident = keep.tile([P, P], BF16, name="ident")
+        make_identity(nc, ident[:])
+        identf = keep.tile([P, P], F32, name="identf")
+        make_identity(nc, identf[:])
+        dummy = keep.tile([P, 1], F32, name="dummy")
+        nc.vector.memset(dummy[:], 0.0)
+        nc.scalar.activation(dummy[:], dummy[:], ACT.Exp)
+
+        kgrp = keep.tile([P, N, PACK], BF16, name="kgrp", tag="grp", align_bytes=64)
+        kcodes = keep.tile([P, N], U32, name="kcodes", align_bytes=64)
+        kscale = keep.tile([P, N], U8, name="kscale", align_bytes=64)
+        vcodes = keep.tile([P, DV], U32, name="vcodes", align_bytes=64)
+        vscale = keep.tile([P, DV], U8, name="vscale", align_bytes=64)
+        qgrp = keep.tile([P, NQ, PACK], BF16, name="qgrp", align_bytes=64)
+        qcodes = keep.tile([P, NQ], U32, name="qcodes", align_bytes=64)
+        qscale = keep.tile([P, NQ], U8, name="qscale", align_bytes=64)
+        ksg = keep.tile([P, N], F32, name="ksg")
+        vsg = keep.tile([P, N], F32, name="vsg")
+        vst = keep.tile([P, PACK], F32, name="vst")
+
+        def write_key(t):
+            nc.vector.tensor_copy(kp[t][:].indirect(place[:]), newk[:, t, :])
+
+        def scalar_key(t):
+            kb = keep.tile([P, T], BF16, name="kb%d" % t)
+            nc.scalar.copy(kb[:], kp[t][:])
+            nc.scalar.activation(kgrp[:, :, t], kb[:].indirect(idx[:]), ACT.Copy)
+
+        write_key(2)
+        scalar_key(2)
+        nc.vector.tensor_copy(ksg[:], ks_sb[:].indirect(idx[:]))
+        write_key(3)
+        scalar_key(3)
+        nc.scalar.copy(qgrp[:], q_sb[:].rearrange("p t q -> p q t"))
+        nc.vector.tensor_copy(vp[0][:].indirect(place[:]), newv[:, 0, :])
+        nc.vector.tensor_copy(vsg[:], vs_sb[:].indirect(idx[:]))
+        vsps = psum.tile([P, PACK, P], F32, name="vsps")
+        for t in range(PACK):
+            nc.tensor.transpose(vsps[:, t, :], vsg[:].rearrange("p (s t) -> p t s", t=PACK)[:, t, :], identf[:])
+        nc.vector.tensor_copy(vp[1][:].indirect(place[:]), newv[:, 1, :])
+        write_key(0)
+        nc.vector.tensor_copy(kgrp[:, :, 0], kp[0][:].indirect(idx[:]))
+        vps = []
+        for b in range(2):
+            vb = keep.tile([P, T], BF16, name="vb%d" % b)
+            vg = keep.tile([P, N], BF16, name="vg%d" % b, align_bytes=64)
+            nc.scalar.copy(vb[:], vp[b][:])
+            nc.scalar.activation(vg[:].rearrange("p (t s) -> p s t", t=PACK), vb[:].indirect(idx[:]), ACT.Copy)
+            vps.append(psum.tile([P, PACK, P], BF16, name="vps%d" % b))
+            for t in range(PACK):
+                nc.tensor.transpose(vps[b][:, t, :], vg[:, t * P : (t + 1) * P], ident[:])
+            if b == 0:
+                nc.scalar.copy(vst[:], vsps[:, :, 0])
+
+        write_key(1)
+        for h in range(2):
+            cols = slice(h * HALF, (h + 1) * HALF)
+            nc.vector.tensor_copy(kgrp[:, cols, 1], kp[1][:].indirect(idx[:, h * HALF // 16 : (h + 1) * HALF // 16]))
+        nc.vector.quantize_mx(out=qcodes[:].bitcast(FP8X4), scales=qscale[:], in_=qgrp[:].rearrange("p q t -> p (q t)"))
+        a = keep.tile([P, PACK, P], F32, name="a")
+        mx2 = keep.tile([P, 2], F32, name="mx2")
+        sc = []
+        for h in range(2):
+            cols = slice(h * HALF, (h + 1) * HALF)
+            sc.append(psum.tile([P, HALF], F32, name="sc%d" % h))
+            nc.vector.quantize_mx(out=kcodes[:, cols].bitcast(FP8X4), scales=kscale[:, cols], in_=kgrp[:, cols, :].rearrange("p n t -> p (n t)"))
+            nc.tensor.matmul_mx(
+                out=sc[h][:],
+                lhsT=qcodes[:].bitcast(FP8X4),
+                lhsT_scale=qscale[:],
+                rhs=kcodes[:, cols].bitcast(FP8X4),
+                rhs_scale=kscale[:, cols],
+                start=True,
+                stop=True,
+            )
+        for h in range(2):
+            cols = slice(h * HALF, (h + 1) * HALF)
+            part = a[:, :, h * 64 : (h + 1) * 64]
+            nc.vector.tensor_tensor(
+                part.rearrange("q t s -> q s t"),
+                sc[h][:].rearrange("q (s t) -> q s t", t=PACK),
+                ksg[:, cols].rearrange("q (s t) -> q s t", t=PACK),
+                ALU.mult,
+            )
+            nc.vector.tensor_reduce(mx2[:, h : h + 1], part, AX.XY, ALU.max)
+        negm = keep.tile([P, 1], F32, name="negm")
+        nc.vector.tensor_reduce(negm[:], mx2[:], AX.X, ALU.max, negate=True)
+
+        p = keep.tile([P, PACK, P], F32, name="p")
+        total2 = keep.tile([P, 2], F32, name="total2")
+        pps = psum.tile([P, PACK, NQ], F32, name="pps")
+        for h in range(2):
+            ts = slice(2 * h, 2 * h + 2)
+            nc.scalar.activation(p[:, ts, :], a[:, ts, :], ACT.Exp, bias=negm[:], scale=1.0, accum_out=total2[:, h : h + 1])
+            for t in range(2 * h, 2 * h + 2):
+                nc.tensor.transpose(pps[:, t, :], p[:, t, :], identf[:])
+
+        vgrp = keep.tile([P, DV, PACK], BF16, name="vgrp", tag="grp", align_bytes=64)
+        for b in range(2):
+            nc.vector.tensor_copy(vgrp[:, b * P : (b + 1) * P, :], vps[b][:].rearrange("s t e -> s e t"))
+        nc.vector.quantize_mx(out=vcodes[:].bitcast(FP8X4), scales=vscale[:], in_=vgrp[:].rearrange("p e t -> p (e t)"))
+
+        wgrp = keep.tile([P, NQ, PACK], BF16, name="wgrp", align_bytes=64)
+        nc.vector.tensor_tensor(wgrp[:], pps[:].rearrange("s t q -> s q t"), vst[:].unsqueeze(1).to_broadcast([P, NQ, PACK]), ALU.mult)
+        wcodes = keep.tile([P, NQ], U32, name="wcodes", align_bytes=64)
+        wscale = keep.tile([P, NQ], U8, name="wscale", align_bytes=64)
+        nc.vector.quantize_mx(out=wcodes[:].bitcast(FP8X4), scales=wscale[:], in_=wgrp[:].rearrange("p q t -> p (q t)"))
+        total = keep.tile([P, 1], F32, name="total")
+        nc.vector.tensor_tensor(total[:], total2[:, 0:1], total2[:, 1:2], ALU.add)
+        recip = keep.tile([P, 1], F32, name="recip")
+        nc.vector.reciprocal(recip[:], total[:])
+        ps_out = psum.tile([P, DV], F32, name="ps_out")
+        nc.tensor.matmul_mx(
+            out=ps_out[:],
+            lhsT=wcodes[:].bitcast(FP8X4),
+            lhsT_scale=wscale[:],
+            rhs=vcodes[:].bitcast(FP8X4),
+            rhs_scale=vscale[:],
+            start=True,
+            stop=True,
+        )
+        o_sb = keep.tile([P, DV], F32, name="o_sb")
+        nc.vector.tensor_scalar(o_sb[:], ps_out[:], recip[:], None, ALU.mult)
+        nc.sync.dma_start(out[0], o_sb[:])

@@ -31,7 +31,9 @@ def tile_attend_x_ks_append128_topk_kernel(tc, qT, kT, vT, new_kT, new_vT, ks, v
         psum = ctx.enter_context(tc.psum_pool(name="psum", bufs=1))
 
         kview = kT.rearrange("(p t) n -> p t n", t=PACK)
-        newk = keep.tile([P, PACK, NEW], F32, name="newk")
+        newkview = new_kT.rearrange("(p t) n -> p t n", t=PACK)
+        newk23 = keep.tile([P, 2, NEW], F32, name="newk23")
+        newk01 = keep.tile([P, 2, NEW], F32, name="newk01")
         newv = keep.tile([P, 2, NEW], F32, name="newv")
         place = keep.tile([P, NEW // 16], U16, name="place")
         idx = keep.tile([P, N // 16], U16, name="idx")
@@ -44,19 +46,20 @@ def tile_attend_x_ks_append128_topk_kernel(tc, qT, kT, vT, new_kT, new_vT, ks, v
         q_sb = keep.tile([P, PACK, NQ], F32, name="q_sb")
         ks_sb = keep.tile([P, T], F32, name="ks_sb")
         vs_sb = keep.tile([P, T], F32, name="vs_sb")
-        nc.sync.dma_start(newk[:], new_kT.rearrange("(p t) n -> p t n", t=PACK))
+        nc.sync.dma_start(newk23[:], newkview[:, 2:4, :])
         nc.sync.dma_start(kp[2][:], kview[:, 2, :])
         nc.sync.dma_start(place[:], slots)
         nc.sync.dma_start(idx[:], offs)
-        nc.sync.dma_start(ks_sb[:], ks)
         nc.sync.dma_start(kp[3][:], kview[:, 3, :])
         nc.sync.dma_start(q_sb[:], qT[0].rearrange("(p t) q -> p t q", t=PACK))
         nc.sync.dma_start(newv[:], new_vT.rearrange("(b p) n -> p b n", b=2))
         nc.sync.dma_start(vp[0][:], vT[0:P, :])
-        nc.sync.dma_start(vs_sb[:], vs)
+        nc.sync.dma_start(ks_sb[:], ks)
         nc.sync.dma_start(vp[1][:], vT[P : 2 * P, :])
+        nc.sync.dma_start(newk01[:], newkview[:, 0:2, :])
         nc.sync.dma_start(kp[0][:], kview[:, 0, :])
         nc.sync.dma_start(kp[1][:], kview[:, 1, :])
+        nc.sync.dma_start(vs_sb[:], vs)
 
         ident = keep.tile([P, P], BF16, name="ident")
         make_identity(nc, ident[:])
@@ -69,17 +72,17 @@ def tile_attend_x_ks_append128_topk_kernel(tc, qT, kT, vT, new_kT, new_vT, ks, v
         kgrp = keep.tile([P, N, PACK], BF16, name="kgrp", tag="grp", align_bytes=64)
         kcodes = keep.tile([P, N], U32, name="kcodes", align_bytes=64)
         kscale = keep.tile([P, N], U8, name="kscale", align_bytes=64)
-        vcodes = keep.tile([P, DV], U32, name="vcodes", align_bytes=64)
+        vgrp = keep.tile([P, DV, PACK], BF16, name="vgrp", align_bytes=64)
         vscale = keep.tile([P, DV], U8, name="vscale", align_bytes=64)
         qgrp = keep.tile([P, NQ, PACK], BF16, name="qgrp", align_bytes=64)
         qcodes = keep.tile([P, NQ], U32, name="qcodes", align_bytes=64)
         qscale = keep.tile([P, NQ], U8, name="qscale", align_bytes=64)
         ksg = keep.tile([P, N], F32, name="ksg")
-        vsg = keep.tile([P, N], F32, name="vsg")
-        vst = keep.tile([P, PACK], F32, name="vst")
+
+        newk = [newk01[:, 0, :], newk01[:, 1, :], newk23[:, 0, :], newk23[:, 1, :]]
 
         def write_key(t):
-            nc.vector.tensor_copy(kp[t][:].indirect(place[:]), newk[:, t, :])
+            nc.vector.tensor_copy(kp[t][:].indirect(place[:]), newk[t])
 
         def scalar_key(t):
             kb = keep.tile([P, T], BF16, name="kb%d" % t)
@@ -88,41 +91,41 @@ def tile_attend_x_ks_append128_topk_kernel(tc, qT, kT, vT, new_kT, new_vT, ks, v
 
         write_key(2)
         scalar_key(2)
-        nc.vector.tensor_copy(ksg[:], ks_sb[:].indirect(idx[:]))
         write_key(3)
         scalar_key(3)
-        nc.scalar.copy(qgrp[:], q_sb[:].rearrange("p t q -> p q t"))
-        nc.vector.tensor_copy(vp[0][:].indirect(place[:]), newv[:, 0, :])
-        nc.vector.tensor_copy(vsg[:], vs_sb[:].indirect(idx[:]))
-        vsps = psum.tile([P, PACK, P], F32, name="vsps")
-        for t in range(PACK):
-            nc.tensor.transpose(vsps[:, t, :], vsg[:].rearrange("p (s t) -> p t s", t=PACK)[:, t, :], identf[:])
-        nc.vector.tensor_copy(vp[1][:].indirect(place[:]), newv[:, 1, :])
-        write_key(0)
-        nc.vector.tensor_copy(kgrp[:, :, 0], kp[0][:].indirect(idx[:]))
-        vps = []
+        nc.vector.tensor_copy(qgrp[:], q_sb[:].rearrange("p t q -> p q t"))
+        nc.vector.quantize_mx(out=qcodes[:].bitcast(FP8X4), scales=qscale[:], in_=qgrp[:].rearrange("p q t -> p (q t)"))
+        vb = []
+        vg = []
         for b in range(2):
-            vb = keep.tile([P, T], BF16, name="vb%d" % b)
-            vg = keep.tile([P, N], BF16, name="vg%d" % b, align_bytes=64)
-            nc.scalar.copy(vb[:], vp[b][:])
-            nc.scalar.activation(vg[:].rearrange("p (t s) -> p s t", t=PACK), vb[:].indirect(idx[:]), ACT.Copy)
-            vps.append(psum.tile([P, PACK, P], BF16, name="vps%d" % b))
-            for t in range(PACK):
-                nc.tensor.transpose(vps[b][:, t, :], vg[:, t * P : (t + 1) * P], ident[:])
-            if b == 0:
-                nc.scalar.copy(vst[:], vsps[:, :, 0])
+            vb.append(keep.tile([P, T], BF16, name="vb%d" % b))
+            vg.append(keep.tile([P, N], BF16, name="vg%d" % b, align_bytes=64))
 
+        def write_value(b):
+            nc.vector.tensor_copy(vp[b][:].indirect(place[:]), newv[:, b, :])
+
+        def scalar_value(b):
+            nc.scalar.copy(vb[b][:], vp[b][:])
+            nc.scalar.activation(vg[b][:].rearrange("p (t s) -> p s t", t=PACK), vb[b][:].indirect(idx[:]), ACT.Copy)
+
+        write_value(0)
+        nc.vector.tensor_copy(ksg[:], ks_sb[:].indirect(idx[:]))
+        write_value(1)
+        write_key(0)
         write_key(1)
+        nc.vector.tensor_copy(kgrp[:, :, 0], kp[0][:].indirect(idx[:]))
         for h in range(2):
             cols = slice(h * HALF, (h + 1) * HALF)
             nc.vector.tensor_copy(kgrp[:, cols, 1], kp[1][:].indirect(idx[:, h * HALF // 16 : (h + 1) * HALF // 16]))
-        nc.vector.quantize_mx(out=qcodes[:].bitcast(FP8X4), scales=qscale[:], in_=qgrp[:].rearrange("p q t -> p (q t)"))
+        for b in range(2):
+            scalar_value(b)
         a = keep.tile([P, PACK, P], F32, name="a")
-        mx2 = keep.tile([P, 2], F32, name="mx2")
+        low = keep.tile([P, 1], F32, name="low")
+        bias = keep.tile([P, 1], F32, name="bias")
         sc = []
         for h in range(2):
             cols = slice(h * HALF, (h + 1) * HALF)
-            sc.append(psum.tile([P, HALF], F32, name="sc%d" % h))
+            sc.append(psum.tile([P, HALF], F32, name="sc%d" % h, tag="scores%d" % h))
             nc.vector.quantize_mx(out=kcodes[:, cols].bitcast(FP8X4), scales=kscale[:, cols], in_=kgrp[:, cols, :].rearrange("p n t -> p (n t)"))
             nc.tensor.matmul_mx(
                 out=sc[h][:],
@@ -133,32 +136,46 @@ def tile_attend_x_ks_append128_topk_kernel(tc, qT, kT, vT, new_kT, new_vT, ks, v
                 start=True,
                 stop=True,
             )
+        vsg = keep.tile([P, N], F32, name="vsg", tag="grp", align_bytes=64)
+        vst = keep.tile([P, PACK], F32, name="vst")
+        nc.vector.tensor_copy(vsg[:], vs_sb[:].indirect(idx[:]))
+        vsps = psum.tile([P, PACK, P], F32, name="vsps")
+        for t in range(PACK):
+            nc.tensor.transpose(vsps[:, t, :], vsg[:].rearrange("p (s t) -> p t s", t=PACK)[:, t, :], identf[:])
+        nc.scalar.copy(vst[:], vsps[:, :, 0])
+        junk = keep.tile([P, PACK, HALF // PACK], F32, name="junk", align_bytes=64)
         for h in range(2):
             cols = slice(h * HALF, (h + 1) * HALF)
             part = a[:, :, h * 64 : (h + 1) * 64]
-            nc.vector.tensor_tensor(
+            nc.vector.scalar_tensor_tensor(
                 part.rearrange("q t s -> q s t"),
                 sc[h][:].rearrange("q (s t) -> q s t", t=PACK),
+                -1.0,
                 ksg[:, cols].rearrange("q (s t) -> q s t", t=PACK),
                 ALU.mult,
+                ALU.mult,
             )
-            nc.vector.tensor_reduce(mx2[:, h : h + 1], part, AX.XY, ALU.max)
-        negm = keep.tile([P, 1], F32, name="negm")
-        nc.vector.tensor_reduce(negm[:], mx2[:], AX.X, ALU.max, negate=True)
+            if h == 0:
+                nc.vector.tensor_reduce(low[:], part, AX.XY, ALU.min)
+            else:
+                nc.vector.tensor_scalar(junk[:], part, 1.0, low[:], ALU.mult, ALU.min, accum_out=bias[:])
 
         p = keep.tile([P, PACK, P], F32, name="p")
         total2 = keep.tile([P, 2], F32, name="total2")
         pps = psum.tile([P, PACK, NQ], F32, name="pps")
         for h in range(2):
             ts = slice(2 * h, 2 * h + 2)
-            nc.scalar.activation(p[:, ts, :], a[:, ts, :], ACT.Exp, bias=negm[:], scale=1.0, accum_out=total2[:, h : h + 1])
-            for t in range(2 * h, 2 * h + 2):
-                nc.tensor.transpose(pps[:, t, :], p[:, t, :], identf[:])
+            nc.scalar.activation(p[:, ts, :], a[:, ts, :], ACT.Exp, bias=bias[:], scale=-1.0, accum_out=total2[:, h : h + 1])
 
-        vgrp = keep.tile([P, DV, PACK], BF16, name="vgrp", tag="grp", align_bytes=64)
+        vps = psum.tile([P, 2, PACK, P], BF16, name="vps", tag="scores1")
         for b in range(2):
-            nc.vector.tensor_copy(vgrp[:, b * P : (b + 1) * P, :], vps[b][:].rearrange("s t e -> s e t"))
+            for t in range(PACK):
+                nc.tensor.transpose(vps[:, b, t, :], vg[b][:, t * P : (t + 1) * P], ident[:])
+        nc.vector.tensor_copy(vgrp[:].rearrange("s (b e) t -> s b e t", b=2), vps[:].rearrange("s b t e -> s b e t"))
+        vcodes = keep.tile([P, DV], U32, name="vcodes", align_bytes=64)
         nc.vector.quantize_mx(out=vcodes[:].bitcast(FP8X4), scales=vscale[:], in_=vgrp[:].rearrange("p e t -> p (e t)"))
+        for t in range(PACK):
+            nc.tensor.transpose(pps[:, t, :], p[:, t, :], identf[:])
 
         wgrp = keep.tile([P, NQ, PACK], BF16, name="wgrp", align_bytes=64)
         nc.vector.tensor_tensor(wgrp[:], pps[:].rearrange("s t q -> s q t"), vst[:].unsqueeze(1).to_broadcast([P, NQ, PACK]), ALU.mult)

from contextlib import ExitStack

import concourse.mybir as mybir
from concourse.masks import make_identity

F32 = mybir.dt.float32
BF16 = mybir.dt.bfloat16
U32 = mybir.dt.uint32
U16 = mybir.dt.uint16
U8 = mybir.dt.uint8
FP8X4 = mybir.dt.float8_e4m3fn_x4
ACT = mybir.ActivationFunctionType
ALU = mybir.AluOpType
AX = mybir.AxisListType

P = 128
PACK = 4
T = 1024
N = 512
NQ = 128
DV = 256
NEW = 128
HALF = N // 2
FLOPS = 2 * NQ * N * 512 + 2 * NQ * N * DV


def tile_attend_x_ks_append128_topk_kernel(tc, qT, kT, vT, new_kT, new_vT, ks, vs, offs, slots, out):
    nc = tc.nc
    with ExitStack() as ctx:
        keep = ctx.enter_context(tc.tile_pool(name="keep", bufs=1))
        psum = ctx.enter_context(tc.psum_pool(name="psum", bufs=1))

        kview = kT.rearrange("(p t) n -> p t n", t=PACK)
        newkview = new_kT.rearrange("(p t) n -> p t n", t=PACK)
        newk23 = keep.tile([P, 2, NEW], F32, name="newk23")
        newk01 = keep.tile([P, 2, NEW], F32, name="newk01")
        newv = keep.tile([P, 2, NEW], F32, name="newv")
        place = keep.tile([P, NEW // 16], U16, name="place")
        idx = keep.tile([P, N // 16], U16, name="idx")
        kp = []
        vp = []
        for t in range(PACK):
            kp.append(keep.tile([P, T], F32, name="kpool%d" % t))
        for b in range(2):
            vp.append(keep.tile([P, T], F32, name="vpool%d" % b))
        q_sb = keep.tile([P, PACK, NQ], F32, name="q_sb")
        ks_sb = keep.tile([P, T], F32, name="ks_sb")
        vs_sb = keep.tile([P, T], F32, name="vs_sb")
        nc.sync.dma_start(newk23[:], newkview[:, 2:4, :])
        nc.sync.dma_start(kp[2][:], kview[:, 2, :])
        nc.sync.dma_start(place[:], slots)
        nc.sync.dma_start(idx[:], offs)
        nc.sync.dma_start(kp[3][:], kview[:, 3, :])
        nc.sync.dma_start(q_sb[:], qT[0].rearrange("(p t) q -> p t q", t=PACK))
        nc.sync.dma_start(newv[:], new_vT.rearrange("(b p) n -> p b n", b=2))
        nc.sync.dma_start(vp[0][:], vT[0:P, :])
        nc.sync.dma_start(ks_sb[:], ks)
        nc.sync.dma_start(vp[1][:], vT[P : 2 * P, :])
        nc.sync.dma_start(newk01[:], newkview[:, 0:2, :])
        nc.sync.dma_start(kp[0][:], kview[:, 0, :])
        nc.sync.dma_start(kp[1][:], kview[:, 1, :])
        nc.sync.dma_start(vs_sb[:], vs)

        ident = keep.tile([P, P], BF16, name="ident")
        make_identity(nc, ident[:])
        identf = keep.tile([P, P], F32, name="identf")
        make_identity(nc, identf[:])
        dummy = keep.tile([P, 1], F32, name="dummy")
        nc.vector.memset(dummy[:], 0.0)
        nc.scalar.activation(dummy[:], dummy[:], ACT.Exp)

        kgrp = keep.tile([P, N, PACK], BF16, name="kgrp", tag="grp", align_bytes=64)
        kcodes = keep.tile([P, N], U32, name="kcodes", align_bytes=64)
        kscale = keep.tile([P, N], U8, name="kscale", align_bytes=64)
        vgrp = keep.tile([P, DV, PACK], BF16, name="vgrp", align_bytes=64)
        vscale = keep.tile([P, DV], U8, name="vscale", align_bytes=64)
        qgrp = keep.tile([P, NQ, PACK], BF16, name="qgrp", align_bytes=64)
        qcodes = keep.tile([P, NQ], U32, name="qcodes", align_bytes=64)
        qscale = keep.tile([P, NQ], U8, name="qscale", align_bytes=64)
        ksg = keep.tile([P, N], F32, name="ksg")

        newk = [newk01[:, 0, :], newk01[:, 1, :], newk23[:, 0, :], newk23[:, 1, :]]

        def write_key(t):
            nc.vector.tensor_copy(kp[t][:].indirect(place[:]), newk[t])

        def scalar_key(t):
            kb = keep.tile([P, T], BF16, name="kb%d" % t)
            nc.scalar.copy(kb[:], kp[t][:])
            nc.scalar.activation(kgrp[:, :, t], kb[:].indirect(idx[:]), ACT.Copy)

        write_key(2)
        scalar_key(2)
        write_key(3)
        scalar_key(3)
        nc.vector.tensor_copy(qgrp[:], q_sb[:].rearrange("p t q -> p q t"))
        nc.vector.quantize_mx(out=qcodes[:].bitcast(FP8X4), scales=qscale[:], in_=qgrp[:].rearrange("p q t -> p (q t)"))
        vb = []
        vg = []
        for b in range(2):
            vb.append(keep.tile([P, T], BF16, name="vb%d" % b))
            vg.append(keep.tile([P, N], BF16, name="vg%d" % b, align_bytes=64))

        def write_value(b):
            nc.vector.tensor_copy(vp[b][:].indirect(place[:]), newv[:, b, :])

        def scalar_value(b):
            nc.scalar.copy(vb[b][:], vp[b][:])
            nc.scalar.activation(vg[b][:].rearrange("p (t s) -> p s t", t=PACK), vb[b][:].indirect(idx[:]), ACT.Copy)

        write_value(0)
        nc.vector.tensor_copy(ksg[:], ks_sb[:].indirect(idx[:]))
        write_value(1)
        write_key(0)
        write_key(1)
        nc.vector.tensor_copy(kgrp[:, :, 0], kp[0][:].indirect(idx[:]))
        for h in range(2):
            cols = slice(h * HALF, (h + 1) * HALF)
            nc.vector.tensor_copy(kgrp[:, cols, 1], kp[1][:].indirect(idx[:, h * HALF // 16 : (h + 1) * HALF // 16]))
        for b in range(2):
            scalar_value(b)
        a = keep.tile([P, PACK, P], F32, name="a")
        low = keep.tile([P, 1], F32, name="low")
        bias = keep.tile([P, 1], F32, name="bias")
        sc = []
        for h in range(2):
            cols = slice(h * HALF, (h + 1) * HALF)
            sc.append(psum.tile([P, HALF], F32, name="sc%d" % h, tag="scores%d" % h))
            nc.vector.quantize_mx(out=kcodes[:, cols].bitcast(FP8X4), scales=kscale[:, cols], in_=kgrp[:, cols, :].rearrange("p n t -> p (n t)"))
            nc.tensor.matmul_mx(
                out=sc[h][:],
                lhsT=qcodes[:].bitcast(FP8X4),
                lhsT_scale=qscale[:],
                rhs=kcodes[:, cols].bitcast(FP8X4),
                rhs_scale=kscale[:, cols],
                start=True,
                stop=True,
            )
        vsg = keep.tile([P, N], F32, name="vsg", tag="grp", align_bytes=64)
        vst = keep.tile([P, PACK], F32, name="vst")
        nc.vector.tensor_copy(vsg[:], vs_sb[:].indirect(idx[:]))
        vsps = psum.tile([P, PACK, P], F32, name="vsps")
        for t in range(PACK):
            nc.tensor.transpose(vsps[:, t, :], vsg[:].rearrange("p (s t) -> p t s", t=PACK)[:, t, :], identf[:])
        nc.scalar.copy(vst[:], vsps[:, :, 0])
        junk = keep.tile([P, PACK, HALF // PACK], F32, name="junk", align_bytes=64)
        for h in range(2):
            cols = slice(h * HALF, (h + 1) * HALF)
            part = a[:, :, h * 64 : (h + 1) * 64]
            nc.vector.scalar_tensor_tensor(
                part.rearrange("q t s -> q s t"),
                sc[h][:].rearrange("q (s t) -> q s t", t=PACK),
                -1.0,
                ksg[:, cols].rearrange("q (s t) -> q s t", t=PACK),
                ALU.mult,
                ALU.mult,
            )
            if h == 0:
                nc.vector.tensor_reduce(low[:], part, AX.XY, ALU.min)
            else:
                nc.vector.tensor_scalar(junk[:], part, 1.0, low[:], ALU.mult, ALU.min, accum_out=bias[:])

        p = keep.tile([P, PACK, P], F32, name="p")
        total2 = keep.tile([P, 2], F32, name="total2")
        pps = psum.tile([P, PACK, NQ], F32, name="pps")
        for h in range(2):
            ts = slice(2 * h, 2 * h + 2)
            nc.scalar.activation(p[:, ts, :], a[:, ts, :], ACT.Exp, bias=bias[:], scale=-1.0, accum_out=total2[:, h : h + 1])

        vps = psum.tile([P, 2, PACK, P], BF16, name="vps", tag="scores1")
        for b in range(2):
            for t in range(PACK):
                nc.tensor.transpose(vps[:, b, t, :], vg[b][:, t * P : (t + 1) * P], ident[:])
        nc.vector.tensor_copy(vgrp[:].rearrange("s (b e) t -> s b e t", b=2), vps[:].rearrange("s b t e -> s b e t"))
        vcodes = keep.tile([P, DV], U32, name="vcodes", align_bytes=64)
        nc.vector.quantize_mx(out=vcodes[:].bitcast(FP8X4), scales=vscale[:], in_=vgrp[:].rearrange("p e t -> p (e t)"))
        for t in range(PACK):
            nc.tensor.transpose(pps[:, t, :], p[:, t, :], identf[:])

        wgrp = keep.tile([P, NQ, PACK], BF16, name="wgrp", align_bytes=64)
        nc.vector.tensor_tensor(wgrp[:], pps[:].rearrange("s t q -> s q t"), vst[:].unsqueeze(1).to_broadcast([P, NQ, PACK]), ALU.mult)
        wcodes = keep.tile([P, NQ], U32, name="wcodes", align_bytes=64)
        wscale = keep.tile([P, NQ], U8, name="wscale", align_bytes=64)
        nc.vector.quantize_mx(out=wcodes[:].bitcast(FP8X4), scales=wscale[:], in_=wgrp[:].rearrange("p q t -> p (q t)"))
        total = keep.tile([P, 1], F32, name="total")
        nc.vector.tensor_tensor(total[:], total2[:, 0:1], total2[:, 1:2], ALU.add)
        recip = keep.tile([P, 1], F32, name="recip")
        nc.vector.reciprocal(recip[:], total[:])
        ps_out = psum.tile([P, DV], F32, name="ps_out")
        nc.tensor.matmul_mx(
            out=ps_out[:],
            lhsT=wcodes[:].bitcast(FP8X4),
            lhsT_scale=wscale[:],
            rhs=vcodes[:].bitcast(FP8X4),
            rhs_scale=vscale[:],
            start=True,
            stop=True,
        )
        o_sb = keep.tile([P, DV], F32, name="o_sb")
        nc.vector.tensor_scalar(o_sb[:], ps_out[:], recip[:], None, ALU.mult)
        nc.sync.dma_start(out[0], o_sb[:])
